import numpy as np
import ml_dtypes


def mxq(x, axis, fmt="e4m3"):
    dtype, down = {"e4m3": (ml_dtypes.float8_e4m3fn, 7), "e5m2": (ml_dtypes.float8_e5m2, 14)}[fmt]
    v = np.moveaxis(np.asarray(x, np.float32).astype(ml_dtypes.bfloat16).astype(np.float64), axis, -1)
    blocks = v.reshape(v.shape[:-1] + (-1, 32))
    amax = np.abs(blocks).max(-1, keepdims=True)
    byte = np.maximum(np.where(amax > 0, np.frexp(amax)[1] - 1 + 127, 0) - down, 1)
    scale = np.exp2(byte - 127.0)
    codes = (blocks / scale).astype(np.float32).astype(dtype).astype(np.float64)
    return np.moveaxis((codes * scale).reshape(v.shape), -1, axis)


WIDE = False


def mx_kscale(k):
    if not WIDE:
        return np.ones(k)
    levels = np.array([10, -10, 5, -5, 0])
    if k % 512:
        return np.exp2(np.random.permutation(np.resize(levels, k // 32))).repeat(32)
    a = np.empty((k // 512, 16))
    for p in range(k // 512):
        a[p, :8] = np.random.permutation(np.resize(levels, 8))
        for g in range(8):
            far = levels[np.abs(levels - a[p, g]) >= 10]
            a[p, g + 8] = far[np.random.randint(len(far))]
    return np.exp2(a.ravel()).repeat(32)


def f64(x):
    return np.asarray(x).astype(np.float64)


def striped(idx):
    return np.tile(idx.reshape(-1, 16).T, (8, 1)).astype(np.uint16)


def unstriped(offs):
    return offs[:16].T.reshape(-1).astype(np.int64)


E2M1 = np.array([0.0, 0.5, 1.0, 1.5, 2.0, 3.0, 4.0, 6.0, -0.0, -0.5, -1.0, -1.5, -2.0, -3.0, -4.0, -6.0])


def pack_weight(w, fmt):
    k, n = w.shape
    w = f64(np.asarray(w, np.float32).astype(ml_dtypes.bfloat16)).reshape(k // 32, 32, n)
    amax = np.abs(w).max(1)
    if fmt == "e4m3":
        byte = np.frexp(amax)[1] - 1 + 127 - 7
    else:
        mant, ex = np.frexp(amax / 6.0)
        byte = np.where(mant > 0.5, ex, ex - 1) + 127
    byte = np.clip(np.where(amax > 0, byte, 1), 1, 254)
    scaled = (w * np.exp2(127.0 - byte)[:, None, :]).reshape(k, n).astype(np.float32)
    by_word = np.ascontiguousarray(scaled.reshape(k // 512, 128, 4, n).transpose(0, 1, 3, 2))
    if fmt == "e4m3":
        words = by_word.astype(ml_dtypes.float8_e4m3fn).view(np.uint8)
    else:
        c = by_word.astype(ml_dtypes.float4_e2m1fn).view(np.uint8) & 0xF
        words = (c[..., 0::2] | (c[..., 1::2] << 4)).reshape(k // 512, 128, 2 * n)
    return np.ascontiguousarray(words), np.ascontiguousarray(byte.astype(np.uint8).reshape(k // 512, 16, n))


def unpack_weight(words, scales, fmt):
    g, _, n = scales.shape
    words = np.ascontiguousarray(words).reshape(g, 128, n, -1)
    if fmt == "e4m3":
        vals = words.view(ml_dtypes.float8_e4m3fn).astype(np.float64)
    else:
        nib = np.empty((g, 128, n, 4), np.uint8)
        nib[..., 0::2] = words & 0xF
        nib[..., 1::2] = words >> 4
        vals = E2M1[nib]
    vals = vals * np.repeat(np.exp2(scales.astype(np.float64) - 127.0), 8, axis=1)[..., None]
    return vals.transpose(0, 1, 3, 2).reshape(g * 512, n)


def pack_table(v):
    words, scales = pack_weight(v, "e4m3")
    return np.concatenate([words.reshape(words.shape[0], -1), scales.reshape(scales.shape[0], -1)], axis=1)


def unpack_table(tab):
    g, t = tab.shape[0], tab.shape[1] // 528
    return unpack_weight(tab[:, :512 * t].reshape(g, 128, t, 4), tab[:, 512 * t:].reshape(g, 16, t), "e4m3")


def split(x):
    m, e = np.frexp(f64(x))
    hi = np.ldexp(np.trunc(16.0 * m) / 16.0, e)
    return hi, f64(x) - hi


def silu(v):
    return v / (1.0 + np.exp(-np.maximum(v, -700.0)))


K, M, T, S = 1536, 256, 512, 256


def setup_inputs():
    n = np.random.standard_normal
    s = mx_kscale(K)[:, None]
    return {
        "tab": pack_table(n((K, T)) * s),
        "w": (n((K, M)) / np.sqrt(K) / s).astype(np.float32),
        "b": (0.3 * n(256)).astype(np.float32),
        "offs": striped(np.random.permutation(T)[:S]),
    }


def reference(tab, w, b, offs):
    tab_ = unpack_table(tab)[:, unstriped(offs)]
    w_hi, w_lo = split(w)
    w_hi_, w_lo_ = mxq(w_hi, 0, "e4m3"), mxq(w_lo, 0, "e4m3")
    y = w_hi_.T @ tab_ + w_lo_.T @ tab_
    return silu(y + f64(b)[:, None])

@@ -1,0 +1,175 @@
+from contextlib import ExitStack
+
+import concourse.mybir as mybir
+
+K, M, T, S = 1536, 256, 512, 256
+FLOPS = 2 * 2 * K * M * S
+
+F32 = mybir.dt.float32
+BF16 = mybir.dt.bfloat16
+I32 = mybir.dt.int32
+U32 = mybir.dt.uint32
+U16 = mybir.dt.uint16
+U8 = mybir.dt.uint8
+FP8X4 = mybir.dt.float8_e4m3fn_x4
+SUBTRACT = mybir.AluOpType.subtract
+AND = mybir.AluOpType.bitwise_and
+SILU = mybir.ActivationFunctionType.Silu
+
+P = 128
+PACK = 4
+K_PASS = P * PACK
+PASSES = K // K_PASS
+M_TILES = M // P
+WORD_BYTES = K_PASS * T
+HI_MASK = -983056
+
+
+def tile_list_tabw_hl_silu_kernel(tc, tab, w, b, offs, out):
+    nc = tc.nc
+    with ExitStack() as ctx:
+        keep = ctx.enter_context(tc.tile_pool(name="keep", bufs=1))
+        psum = ctx.enter_context(tc.psum_pool(name="psum", bufs=1))
+
+        offsets = keep.tile([P, S // 16], U16, name="offsets")
+        nc.sync.dma_start(offsets[:], offs)
+
+        planes = keep.tile([P, T // 4], I32, name="planes", align_bytes=64)
+        nc.vector.memset(planes[:], 0)
+        warm_in = keep.tile([P, 1], F32, name="warm_in")
+        warm_out = keep.tile([P, 1], F32, name="warm_out")
+        nc.vector.memset(warm_in[:], 0.0)
+        nc.scalar.activation(out=warm_out[:], in_=warm_in[:], func=SILU)
+
+        table = [keep.tile([P, T], I32, name=f"table{a}", align_bytes=64) for a in range(PASSES)]
+        raw = [keep.tile([P, PACK, M], F32, name=f"raw{a}", align_bytes=64) for a in range(PASSES)]
+        bias = [keep.tile([P, 1], F32, name=f"bias{m}") for m in range(M_TILES)]
+
+        def load_words(a):
+            nc.sync.dma_start(table[a][:], tab[a, 0:WORD_BYTES].bitcast(I32).rearrange("(p t) -> p t", t=T))
+
+        def load_weights(a):
+            nc.sync.dma_start(raw[a][:], w[a * K_PASS : (a + 1) * K_PASS, :].rearrange("(p j) n -> p j n", j=PACK))
+
+        for q in range(4):
+            first = WORD_BYTES + 4 * q * T
+            nc.gpsimd.dma_start(
+                planes[32 * q : 32 * q + 4 * PASSES, :],
+                tab[:, first : first + 4 * T].bitcast(I32).rearrange("a (r t) -> a r t", r=4),
+            )
+        load_words(0)
+        load_words(1)
+        load_weights(0)
+        load_words(2)
+        load_weights(1)
+        load_weights(2)
+        for m in range(M_TILES):
+            nc.sync.dma_start(bias[m][:], b[m * P : (m + 1) * P].rearrange("(p o) -> p o", o=1))
+
+        words = [keep.tile([P, S], U32, name=f"words{a}", align_bytes=64) for a in range(PASSES)]
+        scales = keep.tile([P, S], U8, name="scales", align_bytes=64)
+
+        def gather_words(a):
+            nc.vector.tensor_copy(words[a][:], table[a][:].bitcast(U32).indirect(offsets[:]))
+
+        def gather_scales():
+            nc.vector.tensor_copy(scales[:], planes[:].bitcast(U8).indirect(offsets[:]))
+
+        cut = [keep.tile([P, M * PACK], BF16, name=f"cut{a}", align_bytes=64) for a in range(PASSES)]
+        high = [keep.tile([P, M * PACK], BF16, name=f"high{a}", align_bytes=64) for a in range(PASSES)]
+        low = [keep.tile([P, M * PACK], BF16, name=f"low{a}", align_bytes=64) for a in range(PASSES)]
+        parts = [[high[a], low[a]] for a in range(PASSES)]
+        codes = [[keep.tile([P, M], U32, name=f"codes{a}_{h}", align_bytes=64) for h in range(2)] for a in range(PASSES)]
+        code_scales = [[keep.tile([P, M], U8, name=f"code_scales{a}_{h}", align_bytes=64) for h in range(2)] for a in range(PASSES)]
+
+        def grouped(tile, c0, c1):
+            return tile[:, c0 * PACK : c1 * PACK].rearrange("p (c i t) -> p c t i", i=4, t=PACK)
+
+        def upper_halves(a, c0, c1):
+            halves = raw[a][:].bitcast(BF16).rearrange("p t (n two) -> p t n two", two=2)
+            return halves[:, :, c0:c1, 1].rearrange("p t (c i) -> p c t i", i=4)
+
+        def pick(a, c0, c1):
+            nc.scalar.copy(out=grouped(cut[a], c0, c1), in_=upper_halves(a, c0, c1))
+
+        def mask(a, c0, c1):
+            nc.vector.tensor_scalar(
+                out=high[a][:, c0 * PACK : c1 * PACK].bitcast(I32),
+                in0=cut[a][:, c0 * PACK : c1 * PACK].bitcast(I32),
+                scalar1=HI_MASK,
+                scalar2=None,
+                op0=AND,
+            )
+
+        def rest(a, c0, c1):
+            nc.vector.tensor_tensor(
+                out=grouped(low[a], c0, c1),
+                in0=raw[a][:, :, c0:c1].rearrange("p t (c i) -> p c t i", i=4),
+                in1=grouped(high[a], c0, c1),
+                op=SUBTRACT,
+            )
+
+        def quantise(a, h, c0, c1):
+            nc.vector.quantize_mx(
+                out=codes[a][h][:, c0:c1].bitcast(FP8X4),
+                scales=code_scales[a][h][:, c0:c1],
+                in_=parts[a][h][:, c0 * PACK : c1 * PACK],
+            )
+
+        acc = [psum.tile([P, S], F32, name=f"acc{m}") for m in range(M_TILES)]
+
+        def multiply(a, h, m):
+            cols = slice(m * P, (m + 1) * P)
+            nc.tensor.matmul_mx(
+                out=acc[m][:],
+                lhsT=codes[a][h][:, cols].bitcast(FP8X4),
+                lhsT_scale=code_scales[a][h][:, cols],
+                rhs=words[a][:].bitcast(FP8X4),
+                rhs_scale=scales[4 * a : P, :],
+                start=(a == 0 and h == 0),
+                stop=(a == PASSES - 1 and h == 1),
+            )
+
+        def finish(m, queue):
+            result = keep.tile([P, S], F32, name=f"result{m}")
+            nc.scalar.activation(out=result[:], in_=acc[m][:], func=SILU, bias=bias[m][:])
+            queue.dma_start(out[m * P : (m + 1) * P, :], result[:])
+
+        gather_words(0)
+        gather_words(1)
+        pick(0, 0, P)
+        pick(0, P, M)
+        gather_scales()
+        gather_words(2)
+        mask(0, 0, M)
+        pick(1, 0, M)
+        rest(0, 0, M)
+        quantise(0, 0, 0, M)
+        multiply(0, 0, 0)
+        multiply(0, 0, 1)
+        mask(1, 0, M)
+        pick(2, 0, P)
+        pick(2, P, M)
+        quantise(0, 1, 0, M)
+        multiply(0, 1, 0)
+        multiply(0, 1, 1)
+        rest(1, 0, M)
+        quantise(1, 0, 0, M)
+        multiply(1, 0, 0)
+        multiply(1, 0, 1)
+        mask(2, 0, P)
+        mask(2, P, M)
+        quantise(1, 1, 0, M)
+        multiply(1, 1, 0)
+        multiply(1, 1, 1)
+        rest(2, 0, P)
+        quantise(2, 0, 0, M)
+        multiply(2, 0, 0)
+        multiply(2, 0, 1)
+        rest(2, P, M)
+        quantise(2, 1, 0, P)
+        multiply(2, 1, 0)
+        finish(0, nc.sync)
+        quantise(2, 1, P, M)
+        multiply(2, 1, 1)
+        finish(1, nc.scalar)

@@ -39,7 +39,6 @@ def tile_list_tabw_hl_silu_kernel(tc, tab, w, b, offs, out):
         warm_in = keep.tile([P, 1], F32, name="warm_in")
         warm_out = keep.tile([P, 1], F32, name="warm_out")
         nc.vector.memset(warm_in[:], 0.0)
-        nc.scalar.activation(out=warm_out[:], in_=warm_in[:], func=SILU)
 
         table = [keep.tile([P, T], I32, name=f"table{a}", align_bytes=64) for a in range(PASSES)]
         raw = [keep.tile([P, PACK, M], F32, name=f"raw{a}", align_bytes=64) for a in range(PASSES)]
@@ -53,14 +52,15 @@ def tile_list_tabw_hl_silu_kernel(tc, tab, w, b, offs, out):
 
         for q in range(4):
             first = WORD_BYTES + 4 * q * T
-            nc.gpsimd.dma_start(
+            nc.scalar.dma_start(
                 planes[32 * q : 32 * q + 4 * PASSES, :],
                 tab[:, first : first + 4 * T].bitcast(I32).rearrange("a (r t) -> a r t", r=4),
             )
+        nc.scalar.activation(out=warm_out[:], in_=warm_in[:], func=SILU)
         load_words(0)
         load_words(1)
-        load_weights(0)
         load_words(2)
+        load_weights(0)
         load_weights(1)
         load_weights(2)
         for m in range(M_TILES):
@@ -76,11 +76,9 @@ def tile_list_tabw_hl_silu_kernel(tc, tab, w, b, offs, out):
             nc.vector.tensor_copy(scales[:], planes[:].bitcast(U8).indirect(offsets[:]))
 
         cut = [keep.tile([P, M * PACK], BF16, name=f"cut{a}", align_bytes=64) for a in range(PASSES)]
-        high = [keep.tile([P, M * PACK], BF16, name=f"high{a}", align_bytes=64) for a in range(PASSES)]
-        low = [keep.tile([P, M * PACK], BF16, name=f"low{a}", align_bytes=64) for a in range(PASSES)]
-        parts = [[high[a], low[a]] for a in range(PASSES)]
-        codes = [[keep.tile([P, M], U32, name=f"codes{a}_{h}", align_bytes=64) for h in range(2)] for a in range(PASSES)]
-        code_scales = [[keep.tile([P, M], U8, name=f"code_scales{a}_{h}", align_bytes=64) for h in range(2)] for a in range(PASSES)]
+        parts = [keep.tile([P, 2 * M * PACK], BF16, name=f"parts{a}", align_bytes=64) for a in range(PASSES)]
+        codes = [keep.tile([P, 2 * M], U32, name=f"codes{a}", align_bytes=64) for a in range(PASSES)]
+        code_scales = [keep.tile([P, 2 * M], U8, name=f"code_scales{a}", align_bytes=64) for a in range(PASSES)]
 
         def grouped(tile, c0, c1):
             return tile[:, c0 * PACK : c1 * PACK].rearrange("p (c i t) -> p c t i", i=4, t=PACK)
@@ -94,7 +92,7 @@ def tile_list_tabw_hl_silu_kernel(tc, tab, w, b, offs, out):
 
         def mask(a, c0, c1):
             nc.vector.tensor_scalar(
-                out=high[a][:, c0 * PACK : c1 * PACK].bitcast(I32),
+                out=parts[a][:, c0 * PACK : c1 * PACK].bitcast(I32),
                 in0=cut[a][:, c0 * PACK : c1 * PACK].bitcast(I32),
                 scalar1=HI_MASK,
                 scalar2=None,
@@ -103,27 +101,27 @@ def tile_list_tabw_hl_silu_kernel(tc, tab, w, b, offs, out):
 
         def rest(a, c0, c1):
             nc.vector.tensor_tensor(
-                out=grouped(low[a], c0, c1),
+                out=grouped(parts[a], M + c0, M + c1),
                 in0=raw[a][:, :, c0:c1].rearrange("p t (c i) -> p c t i", i=4),
-                in1=grouped(high[a], c0, c1),
+                in1=grouped(parts[a], c0, c1),
                 op=SUBTRACT,
             )
 
-        def quantise(a, h, c0, c1):
+        def quantise(a, c0, c1):
             nc.vector.quantize_mx(
-                out=codes[a][h][:, c0:c1].bitcast(FP8X4),
-                scales=code_scales[a][h][:, c0:c1],
-                in_=parts[a][h][:, c0 * PACK : c1 * PACK],
+                out=codes[a][:, c0:c1].bitcast(FP8X4),
+                scales=code_scales[a][:, c0:c1],
+                in_=parts[a][:, c0 * PACK : c1 * PACK],
             )
 
         acc = [psum.tile([P, S], F32, name=f"acc{m}") for m in range(M_TILES)]
 
         def multiply(a, h, m):
-            cols = slice(m * P, (m + 1) * P)
+            cols = slice(h * M + m * P, h * M + (m + 1) * P)
             nc.tensor.matmul_mx(
                 out=acc[m][:],
-                lhsT=codes[a][h][:, cols].bitcast(FP8X4),
-                lhsT_scale=code_scales[a][h][:, cols],
+                lhsT=codes[a][:, cols].bitcast(FP8X4),
+                lhsT_scale=code_scales[a][:, cols],
                 rhs=words[a][:].bitcast(FP8X4),
                 rhs_scale=scales[4 * a : P, :],
                 start=(a == 0 and h == 0),
@@ -135,41 +133,38 @@ def tile_list_tabw_hl_silu_kernel(tc, tab, w, b, offs, out):
             nc.scalar.activation(out=result[:], in_=acc[m][:], func=SILU, bias=bias[m][:])
             queue.dma_start(out[m * P : (m + 1) * P, :], result[:])
 
-        gather_words(0)
-        gather_words(1)
         pick(0, 0, P)
         pick(0, P, M)
-        gather_scales()
+        gather_words(0)
+        gather_words(1)
         gather_words(2)
-        mask(0, 0, M)
+        mask(0, 0, P)
+        rest(0, 0, P)
+        mask(0, P, M)
         pick(1, 0, M)
-        rest(0, 0, M)
-        quantise(0, 0, 0, M)
-        multiply(0, 0, 0)
-        multiply(0, 0, 1)
+        rest(0, P, M)
+        gather_scales()
         mask(1, 0, M)
+        quantise(0, 0, 2 * M)
+        for h in range(2):
+            for m in range(M_TILES):
+                multiply(0, h, m)
         pick(2, 0, P)
         pick(2, P, M)
-        quantise(0, 1, 0, M)
-        multiply(0, 1, 0)
-        multiply(0, 1, 1)
         rest(1, 0, M)
-        quantise(1, 0, 0, M)
-        multiply(1, 0, 0)
-        multiply(1, 0, 1)
-        mask(2, 0, P)
-        mask(2, P, M)
-        quantise(1, 1, 0, M)
-        multiply(1, 1, 0)
-        multiply(1, 1, 1)
+        mask(2, 0, M)
+        quantise(1, 0, 2 * M)
+        for h in range(2):
+            for m in range(M_TILES):
+                multiply(1, h, m)
         rest(2, 0, P)
-        quantise(2, 0, 0, M)
+        quantise(2, 0, M)
         multiply(2, 0, 0)
         multiply(2, 0, 1)
         rest(2, P, M)
-        quantise(2, 1, 0, P)
+        quantise(2, M, M + P)
         multiply(2, 1, 0)
         finish(0, nc.sync)
-        quantise(2, 1, P, M)
+        quantise(2, M + P, 2 * M)
         multiply(2, 1, 1)
         finish(1, nc.scalar)

@@ -22,6 +22,7 @@ K_PASS = P * PACK
 PASSES = K // K_PASS
 M_TILES = M // P
 WORD_BYTES = K_PASS * T
+RUNS = [[(0, P), (P, M)], [(0, M)], [(0, M)]]
 HI_MASK = -983056
 
 
@@ -41,27 +42,35 @@ def tile_list_tabw_hl_silu_kernel(tc, tab, w, b, offs, out):
         nc.vector.memset(warm_in[:], 0.0)
 
         table = [keep.tile([P, T], I32, name=f"table{a}", align_bytes=64) for a in range(PASSES)]
-        raw = [keep.tile([P, PACK, M], F32, name=f"raw{a}", align_bytes=64) for a in range(PASSES)]
+        raw = [[keep.tile([P, PACK, n1 - n0], F32, name=f"raw{a}_{n0}", align_bytes=64) for n0, n1 in RUNS[a]] for a in range(PASSES)]
         bias = [keep.tile([P, 1], F32, name=f"bias{m}") for m in range(M_TILES)]
 
         def load_words(a):
             nc.sync.dma_start(table[a][:], tab[a, 0:WORD_BYTES].bitcast(I32).rearrange("(p t) -> p t", t=T))
 
         def load_weights(a):
-            nc.sync.dma_start(raw[a][:], w[a * K_PASS : (a + 1) * K_PASS, :].rearrange("(p j) n -> p j n", j=PACK))
+            rows = w[a * K_PASS : (a + 1) * K_PASS, :].rearrange("(p j) n -> p j n", j=PACK)
+            for r, (n0, n1) in enumerate(RUNS[a]):
+                nc.sync.dma_start(raw[a][r][:], rows[:, :, n0:n1])
 
-        for q in range(4):
-            first = WORD_BYTES + 4 * q * T
-            nc.scalar.dma_start(
-                planes[32 * q : 32 * q + 4 * PASSES, :],
-                tab[:, first : first + 4 * T].bitcast(I32).rearrange("a (r t) -> a r t", r=4),
-            )
+        def raw_columns(a, c0, c1):
+            for r, (n0, n1) in enumerate(RUNS[a]):
+                if n0 <= c0 and c1 <= n1:
+                    return raw[a][r], c0 - n0, c1 - n0
+            return None
+
         nc.scalar.activation(out=warm_out[:], in_=warm_in[:], func=SILU)
         load_words(0)
         load_words(1)
         load_words(2)
         load_weights(0)
         load_weights(1)
+        for q in range(4):
+            first = WORD_BYTES + 4 * q * T
+            nc.sync.dma_start(
+                planes[32 * q : 32 * q + 4 * PASSES, :],
+                tab[:, first : first + 4 * T].bitcast(I32).rearrange("a (r t) -> a r t", r=4),
+            )
         load_weights(2)
         for m in range(M_TILES):
             nc.sync.dma_start(bias[m][:], b[m * P : (m + 1) * P].rearrange("(p o) -> p o", o=1))
@@ -84,8 +93,9 @@ def tile_list_tabw_hl_silu_kernel(tc, tab, w, b, offs, out):
             return tile[:, c0 * PACK : c1 * PACK].rearrange("p (c i t) -> p c t i", i=4, t=PACK)
 
         def upper_halves(a, c0, c1):
-            halves = raw[a][:].bitcast(BF16).rearrange("p t (n two) -> p t n two", two=2)
-            return halves[:, :, c0:c1, 1].rearrange("p t (c i) -> p c t i", i=4)
+            tile, d0, d1 = raw_columns(a, c0, c1)
+            halves = tile[:].bitcast(BF16).rearrange("p t (n two) -> p t n two", two=2)
+            return halves[:, :, d0:d1, 1].rearrange("p t (c i) -> p c t i", i=4)
 
         def pick(a, c0, c1):
             nc.scalar.copy(out=grouped(cut[a], c0, c1), in_=upper_halves(a, c0, c1))
@@ -100,9 +110,10 @@ def tile_list_tabw_hl_silu_kernel(tc, tab, w, b, offs, out):
             )
 
         def rest(a, c0, c1):
+            tile, d0, d1 = raw_columns(a, c0, c1)
             nc.vector.tensor_tensor(
                 out=grouped(parts[a], M + c0, M + c1),
-                in0=raw[a][:, :, c0:c1].rearrange("p t (c i) -> p c t i", i=4),
+                in0=tile[:, :, d0:d1].rearrange("p t (c i) -> p c t i", i=4),
                 in1=grouped(parts[a], c0, c1),
                 op=SUBTRACT,
             )
@@ -143,16 +154,16 @@ def tile_list_tabw_hl_silu_kernel(tc, tab, w, b, offs, out):
         mask(0, P, M)
         pick(1, 0, M)
         rest(0, P, M)
-        gather_scales()
         mask(1, 0, M)
         quantise(0, 0, 2 * M)
-        for h in range(2):
-            for m in range(M_TILES):
-                multiply(0, h, m)
         pick(2, 0, P)
         pick(2, P, M)
         rest(1, 0, M)
         mask(2, 0, M)
+        gather_scales()
+        for h in range(2):
+            for m in range(M_TILES):
+                multiply(0, h, m)
         quantise(1, 0, 2 * M)
         for h in range(2):
             for m in range(M_TILES):

@@ -23,6 +23,7 @@ PASSES = K // K_PASS
 M_TILES = M // P
 WORD_BYTES = K_PASS * T
 RUNS = [[(0, P), (P, M)], [(0, M)], [(0, M)]]
+WORD_MASK = -1048576
 HI_MASK = -983056
 
 
@@ -48,10 +49,10 @@ def tile_list_tabw_hl_silu_kernel(tc, tab, w, b, offs, out):
         def load_words(a):
             nc.sync.dma_start(table[a][:], tab[a, 0:WORD_BYTES].bitcast(I32).rearrange("(p t) -> p t", t=T))
 
-        def load_weights(a):
+        def load_weights(a, r):
             rows = w[a * K_PASS : (a + 1) * K_PASS, :].rearrange("(p j) n -> p j n", j=PACK)
-            for r, (n0, n1) in enumerate(RUNS[a]):
-                nc.sync.dma_start(raw[a][r][:], rows[:, :, n0:n1])
+            n0, n1 = RUNS[a][r]
+            nc.sync.dma_start(raw[a][r][:], rows[:, :, n0:n1])
 
         def raw_columns(a, c0, c1):
             for r, (n0, n1) in enumerate(RUNS[a]):
@@ -61,17 +62,18 @@ def tile_list_tabw_hl_silu_kernel(tc, tab, w, b, offs, out):
 
         nc.scalar.activation(out=warm_out[:], in_=warm_in[:], func=SILU)
         load_words(0)
+        load_weights(0, 0)
         load_words(1)
+        load_weights(0, 1)
         load_words(2)
-        load_weights(0)
-        load_weights(1)
+        load_weights(1, 0)
         for q in range(4):
             first = WORD_BYTES + 4 * q * T
             nc.sync.dma_start(
                 planes[32 * q : 32 * q + 4 * PASSES, :],
                 tab[:, first : first + 4 * T].bitcast(I32).rearrange("a (r t) -> a r t", r=4),
             )
-        load_weights(2)
+        load_weights(2, 0)
         for m in range(M_TILES):
             nc.sync.dma_start(bias[m][:], b[m * P : (m + 1) * P].rearrange("(p o) -> p o", o=1))
 
@@ -96,6 +98,27 @@ def tile_list_tabw_hl_silu_kernel(tc, tab, w, b, offs, out):
             tile, d0, d1 = raw_columns(a, c0, c1)
             halves = tile[:].bitcast(BF16).rearrange("p t (n two) -> p t n two", two=2)
             return halves[:, :, d0:d1, 1].rearrange("p t (c i) -> p c t i", i=4)
+
+        first_high = keep.tile([P, PACK, P], F32, name="first_high", align_bytes=64)
+
+        def mask_first():
+            nc.vector.tensor_scalar(
+                out=first_high[:].bitcast(I32), in0=raw[0][0][:].bitcast(I32), scalar1=WORD_MASK, scalar2=None, op0=AND
+            )
+
+        def pick_first():
+            halves = first_high[:].bitcast(BF16).rearrange("p t (n two) -> p t n two", two=2)
+            nc.scalar.copy(
+                out=grouped(parts[0], 0, P), in_=halves[:, :, :, 1].rearrange("p t (c i) -> p c t i", i=4)
+            )
+
+        def rest_first():
+            nc.vector.tensor_tensor(
+                out=grouped(parts[0], M, M + P),
+                in0=raw[0][0][:].rearrange("p t (c i) -> p c t i", i=4),
+                in1=first_high[:].rearrange("p t (c i) -> p c t i", i=4),
+                op=SUBTRACT,
+            )
 
         def pick(a, c0, c1):
             nc.scalar.copy(out=grouped(cut[a], c0, c1), in_=upper_halves(a, c0, c1))
@@ -144,26 +167,29 @@ def tile_list_tabw_hl_silu_kernel(tc, tab, w, b, offs, out):
             nc.scalar.activation(out=result[:], in_=acc[m][:], func=SILU, bias=bias[m][:])
             queue.dma_start(out[m * P : (m + 1) * P, :], result[:])
 
-        pick(0, 0, P)
-        pick(0, P, M)
         gather_words(0)
+        mask_first()
+        pick_first()
         gather_words(1)
-        gather_words(2)
-        mask(0, 0, P)
-        rest(0, 0, P)
+        rest_first()
+        pick(0, P, M)
         mask(0, P, M)
-        pick(1, 0, M)
+        gather_words(2)
         rest(0, P, M)
-        mask(1, 0, M)
-        quantise(0, 0, 2 * M)
-        pick(2, 0, P)
-        pick(2, P, M)
-        rest(1, 0, M)
-        mask(2, 0, M)
+        pick(1, 0, P)
+        pick(1, P, M)
+        quantise(0, 0, M)
+        mask(1, 0, P)
+        quantise(0, M, 2 * M)
+        mask(1, P, M)
         gather_scales()
         for h in range(2):
             for m in range(M_TILES):
                 multiply(0, h, m)
+        rest(1, 0, M)
+        pick(2, 0, P)
+        pick(2, P, M)
+        mask(2, 0, M)
         quantise(1, 0, 2 * M)
         for h in range(2):
             for m in range(M_TILES):

@@ -22,7 +22,6 @@ K_PASS = P * PACK
 PASSES = K // K_PASS
 M_TILES = M // P
 WORD_BYTES = K_PASS * T
-RUNS = [[(0, P), (P, M)], [(0, M)], [(0, M)]]
 WORD_MASK = -1048576
 HI_MASK = -983056
 
@@ -43,37 +42,33 @@ def tile_list_tabw_hl_silu_kernel(tc, tab, w, b, offs, out):
         nc.vector.memset(warm_in[:], 0.0)
 
         table = [keep.tile([P, T], I32, name=f"table{a}", align_bytes=64) for a in range(PASSES)]
-        raw = [[keep.tile([P, PACK, n1 - n0], F32, name=f"raw{a}_{n0}", align_bytes=64) for n0, n1 in RUNS[a]] for a in range(PASSES)]
+        raw = [keep.tile([P, PACK, M], F32, name=f"raw{a}", align_bytes=64) for a in range(PASSES)]
         bias = [keep.tile([P, 1], F32, name=f"bias{m}") for m in range(M_TILES)]
 
-        def load_words(a):
-            nc.sync.dma_start(table[a][:], tab[a, 0:WORD_BYTES].bitcast(I32).rearrange("(p t) -> p t", t=T))
+        def load_words(a, queue):
+            queue.dma_start(table[a][:], tab[a, 0:WORD_BYTES].bitcast(I32).rearrange("(p t) -> p t", t=T))
 
-        def load_weights(a, r):
-            rows = w[a * K_PASS : (a + 1) * K_PASS, :].rearrange("(p j) n -> p j n", j=PACK)
-            n0, n1 = RUNS[a][r]
-            nc.sync.dma_start(raw[a][r][:], rows[:, :, n0:n1])
+        def load_weights(a):
+            nc.sync.dma_start(raw[a][:], w[a * K_PASS : (a + 1) * K_PASS, :].rearrange("(p j) n -> p j n", j=PACK))
 
-        def raw_columns(a, c0, c1):
-            for r, (n0, n1) in enumerate(RUNS[a]):
-                if n0 <= c0 and c1 <= n1:
-                    return raw[a][r], c0 - n0, c1 - n0
-            return None
-
-        nc.scalar.activation(out=warm_out[:], in_=warm_in[:], func=SILU)
-        load_words(0)
-        load_weights(0, 0)
-        load_words(1)
-        load_weights(0, 1)
-        load_words(2)
-        load_weights(1, 0)
-        for q in range(4):
+        def load_scales(q, queue):
             first = WORD_BYTES + 4 * q * T
-            nc.sync.dma_start(
+            queue.dma_start(
                 planes[32 * q : 32 * q + 4 * PASSES, :],
                 tab[:, first : first + 4 * T].bitcast(I32).rearrange("a (r t) -> a r t", r=4),
             )
-        load_weights(2, 0)
+
+        load_scales(0, nc.gpsimd)
+        load_scales(1, nc.gpsimd)
+        load_words(0, nc.sync)
+        load_words(1, nc.sync)
+        load_weights(0)
+        load_words(2, nc.sync)
+        load_scales(2, nc.sync)
+        load_scales(3, nc.sync)
+        nc.scalar.activation(out=warm_out[:], in_=warm_in[:], func=SILU)
+        load_weights(1)
+        load_weights(2)
         for m in range(M_TILES):
             nc.sync.dma_start(bias[m][:], b[m * P : (m + 1) * P].rearrange("(p o) -> p o", o=1))
 
@@ -95,15 +90,14 @@ def tile_list_tabw_hl_silu_kernel(tc, tab, w, b, offs, out):
             return tile[:, c0 * PACK : c1 * PACK].rearrange("p (c i t) -> p c t i", i=4, t=PACK)
 
         def upper_halves(a, c0, c1):
-            tile, d0, d1 = raw_columns(a, c0, c1)
-            halves = tile[:].bitcast(BF16).rearrange("p t (n two) -> p t n two", two=2)
-            return halves[:, :, d0:d1, 1].rearrange("p t (c i) -> p c t i", i=4)
+            halves = raw[a][:].bitcast(BF16).rearrange("p t (n two) -> p t n two", two=2)
+            return halves[:, :, c0:c1, 1].rearrange("p t (c i) -> p c t i", i=4)
 
         first_high = keep.tile([P, PACK, P], F32, name="first_high", align_bytes=64)
 
         def mask_first():
             nc.vector.tensor_scalar(
-                out=first_high[:].bitcast(I32), in0=raw[0][0][:].bitcast(I32), scalar1=WORD_MASK, scalar2=None, op0=AND
+                out=first_high[:].bitcast(I32), in0=raw[0][:].bitcast(I32)[:, :, 0:P], scalar1=WORD_MASK, scalar2=None, op0=AND
             )
 
         def pick_first():
@@ -115,7 +109,7 @@ def tile_list_tabw_hl_silu_kernel(tc, tab, w, b, offs, out):
         def rest_first():
             nc.vector.tensor_tensor(
                 out=grouped(parts[0], M, M + P),
-                in0=raw[0][0][:].rearrange("p t (c i) -> p c t i", i=4),
+                in0=raw[0][:, :, 0:P].rearrange("p t (c i) -> p c t i", i=4),
                 in1=first_high[:].rearrange("p t (c i) -> p c t i", i=4),
                 op=SUBTRACT,
             )
@@ -133,10 +127,9 @@ def tile_list_tabw_hl_silu_kernel(tc, tab, w, b, offs, out):
             )
 
         def rest(a, c0, c1):
-            tile, d0, d1 = raw_columns(a, c0, c1)
             nc.vector.tensor_tensor(
                 out=grouped(parts[a], M + c0, M + c1),
-                in0=tile[:, :, d0:d1].rearrange("p t (c i) -> p c t i", i=4),
+                in0=raw[a][:, :, c0:c1].rearrange("p t (c i) -> p c t i", i=4),
                 in1=grouped(parts[a], c0, c1),
                 op=SUBTRACT,
             )
@@ -168,12 +161,12 @@ def tile_list_tabw_hl_silu_kernel(tc, tab, w, b, offs, out):
             queue.dma_start(out[m * P : (m + 1) * P, :], result[:])
 
         gather_words(0)
-        mask_first()
-        pick_first()
         gather_words(1)
-        rest_first()
+        mask_first()
         pick(0, P, M)
+        pick_first()
         mask(0, P, M)
+        rest_first()
         gather_words(2)
         rest(0, P, M)
         pick(1, 0, P)

from contextlib import ExitStack

import concourse.mybir as mybir

K, M, T, S = 1536, 256, 512, 256
FLOPS = 2 * 2 * K * M * S

F32 = mybir.dt.float32
BF16 = mybir.dt.bfloat16
I32 = mybir.dt.int32
U32 = mybir.dt.uint32
U16 = mybir.dt.uint16
U8 = mybir.dt.uint8
FP8X4 = mybir.dt.float8_e4m3fn_x4
SUBTRACT = mybir.AluOpType.subtract
AND = mybir.AluOpType.bitwise_and
SILU = mybir.ActivationFunctionType.Silu

P = 128
PACK = 4
K_PASS = P * PACK
PASSES = K // K_PASS
M_TILES = M // P
WORD_BYTES = K_PASS * T
WORD_MASK = -1048576
HI_MASK = -983056


def tile_list_tabw_hl_silu_kernel(tc, tab, w, b, offs, out):
    nc = tc.nc
    with ExitStack() as ctx:
        keep = ctx.enter_context(tc.tile_pool(name="keep", bufs=1))
        psum = ctx.enter_context(tc.psum_pool(name="psum", bufs=1))

        offsets = keep.tile([P, S // 16], U16, name="offsets")
        nc.sync.dma_start(offsets[:], offs)

        planes = keep.tile([P, T // 4], I32, name="planes", align_bytes=64)
        nc.vector.memset(planes[:], 0)
        warm_in = keep.tile([P, 1], F32, name="warm_in")
        warm_out = keep.tile([P, 1], F32, name="warm_out")
        nc.vector.memset(warm_in[:], 0.0)

        table = [keep.tile([P, T], I32, name=f"table{a}", align_bytes=64) for a in range(PASSES)]
        raw = [keep.tile([P, PACK, M], F32, name=f"raw{a}", align_bytes=64) for a in range(PASSES)]
        bias = [keep.tile([P, 1], F32, name=f"bias{m}") for m in range(M_TILES)]

        def load_words(a, queue):
            queue.dma_start(table[a][:], tab[a, 0:WORD_BYTES].bitcast(I32).rearrange("(p t) -> p t", t=T))

        def load_weights(a):
            nc.sync.dma_start(raw[a][:], w[a * K_PASS : (a + 1) * K_PASS, :].rearrange("(p j) n -> p j n", j=PACK))

        def load_scales(q, queue):
            first = WORD_BYTES + 4 * q * T
            queue.dma_start(
                planes[32 * q : 32 * q + 4 * PASSES, :],
                tab[:, first : first + 4 * T].bitcast(I32).rearrange("a (r t) -> a r t", r=4),
            )

        load_scales(0, nc.gpsimd)
        load_scales(1, nc.gpsimd)
        load_words(0, nc.sync)
        load_words(1, nc.sync)
        load_weights(0)
        load_words(2, nc.sync)
        load_scales(2, nc.sync)
        load_scales(3, nc.sync)
        nc.scalar.activation(out=warm_out[:], in_=warm_in[:], func=SILU)
        load_weights(1)
        load_weights(2)
        for m in range(M_TILES):
            nc.sync.dma_start(bias[m][:], b[m * P : (m + 1) * P].rearrange("(p o) -> p o", o=1))

        words = [keep.tile([P, S], U32, name=f"words{a}", align_bytes=64) for a in range(PASSES)]
        scales = keep.tile([P, S], U8, name="scales", align_bytes=64)

        def gather_words(a):
            nc.vector.tensor_copy(words[a][:], table[a][:].bitcast(U32).indirect(offsets[:]))

        def gather_scales():
            nc.vector.tensor_copy(scales[:], planes[:].bitcast(U8).indirect(offsets[:]))

        cut = [keep.tile([P, M * PACK], BF16, name=f"cut{a}", align_bytes=64) for a in range(PASSES)]
        parts = [keep.tile([P, 2 * M * PACK], BF16, name=f"parts{a}", align_bytes=64) for a in range(PASSES)]
        codes = [keep.tile([P, 2 * M], U32, name=f"codes{a}", align_bytes=64) for a in range(PASSES)]
        code_scales = [keep.tile([P, 2 * M], U8, name=f"code_scales{a}", align_bytes=64) for a in range(PASSES)]

        def grouped(tile, c0, c1):
            return tile[:, c0 * PACK : c1 * PACK].rearrange("p (c i t) -> p c t i", i=4, t=PACK)

        def upper_halves(a, c0, c1):
            halves = raw[a][:].bitcast(BF16).rearrange("p t (n two) -> p t n two", two=2)
            return halves[:, :, c0:c1, 1].rearrange("p t (c i) -> p c t i", i=4)

        first_high = keep.tile([P, PACK, P], F32, name="first_high", align_bytes=64)

        def mask_first():
            nc.vector.tensor_scalar(
                out=first_high[:].bitcast(I32), in0=raw[0][:].bitcast(I32)[:, :, 0:P], scalar1=WORD_MASK, scalar2=None, op0=AND
            )

        def pick_first():
            halves = first_high[:].bitcast(BF16).rearrange("p t (n two) -> p t n two", two=2)
            nc.scalar.copy(
                out=grouped(parts[0], 0, P), in_=halves[:, :, :, 1].rearrange("p t (c i) -> p c t i", i=4)
            )

        def rest_first():
            nc.vector.tensor_tensor(
                out=grouped(parts[0], M, M + P),
                in0=raw[0][:, :, 0:P].rearrange("p t (c i) -> p c t i", i=4),
                in1=first_high[:].rearrange("p t (c i) -> p c t i", i=4),
                op=SUBTRACT,
            )

        def pick(a, c0, c1):
            nc.scalar.copy(out=grouped(cut[a], c0, c1), in_=upper_halves(a, c0, c1))

        def mask(a, c0, c1):
            nc.vector.tensor_scalar(
                out=parts[a][:, c0 * PACK : c1 * PACK].bitcast(I32),
                in0=cut[a][:, c0 * PACK : c1 * PACK].bitcast(I32),
                scalar1=HI_MASK,
                scalar2=None,
                op0=AND,
            )

        def rest(a, c0, c1):
            nc.vector.tensor_tensor(
                out=grouped(parts[a], M + c0, M + c1),
                in0=raw[a][:, :, c0:c1].rearrange("p t (c i) -> p c t i", i=4),
                in1=grouped(parts[a], c0, c1),
                op=SUBTRACT,
            )

        def quantise(a, c0, c1):
            nc.vector.quantize_mx(
                out=codes[a][:, c0:c1].bitcast(FP8X4),
                scales=code_scales[a][:, c0:c1],
                in_=parts[a][:, c0 * PACK : c1 * PACK],
            )

        acc = [psum.tile([P, S], F32, name=f"acc{m}") for m in range(M_TILES)]

        def multiply(a, h, m):
            cols = slice(h * M + m * P, h * M + (m + 1) * P)
            nc.tensor.matmul_mx(
                out=acc[m][:],
                lhsT=codes[a][:, cols].bitcast(FP8X4),
                lhsT_scale=code_scales[a][:, cols],
                rhs=words[a][:].bitcast(FP8X4),
                rhs_scale=scales[4 * a : P, :],
                start=(a == 0 and h == 0),
                stop=(a == PASSES - 1 and h == 1),
            )

        def finish(m, queue):
            result = keep.tile([P, S], F32, name=f"result{m}")
            nc.scalar.activation(out=result[:], in_=acc[m][:], func=SILU, bias=bias[m][:])
            queue.dma_start(out[m * P : (m + 1) * P, :], result[:])

        gather_words(0)
        gather_words(1)
        mask_first()
        pick(0, P, M)
        pick_first()
        mask(0, P, M)
        rest_first()
        gather_words(2)
        rest(0, P, M)
        pick(1, 0, P)
        pick(1, P, M)
        quantise(0, 0, M)
        mask(1, 0, P)
        quantise(0, M, 2 * M)
        mask(1, P, M)
        gather_scales()
        for h in range(2):
            for m in range(M_TILES):
                multiply(0, h, m)
        rest(1, 0, M)
        pick(2, 0, P)
        pick(2, P, M)
        mask(2, 0, M)
        quantise(1, 0, 2 * M)
        for h in range(2):
            for m in range(M_TILES):
                multiply(1, h, m)
        rest(2, 0, P)
        quantise(2, 0, M)
        multiply(2, 0, 0)
        multiply(2, 0, 1)
        rest(2, P, M)
        quantise(2, M, M + P)
        multiply(2, 1, 0)
        finish(0, nc.sync)
        quantise(2, M + P, 2 * M)
        multiply(2, 1, 1)
        finish(1, nc.scalar)
